import numpy as np
CORES = [23,39,55,63,87,103,111,127,18,34,50,58,82,98,106,122]
N = 16
R, W, T = 4096, 64, 256
def entries(a): return a.T.reshape(-1)
def pack(v, P): return np.ascontiguousarray(np.asarray(v, np.int32).reshape(-1, P).T)
def lists(rng, how):
    I = rng.integers(0, N * R, (N, T))
    if how == "alike": I[:] = rng.integers(0, N * R, (N, 1))
    if how == "distinct": I = np.stack([rng.permutation(N * R)[:T] for r in range(N)])
    if how == "hotrank": I = R * int(rng.integers(N)) + rng.integers(0, R, (N, T))
    if how == "own": I = R * np.arange(N).reshape(N, 1) + rng.integers(0, R, (N, T))
    if how == "edge": I = R * rng.integers(0, N, (N, T)) + np.where(rng.random((N, T)) < 0.5, 0, R - 1)
    return {"idx": np.stack([pack(I[r], 128) for r in range(N)])}
def setup_inputs(rng):
    return dict({"tab": rng.standard_normal((N, R, W), dtype=np.float32)}, **lists(rng, "uniform"))
def setup_inputs_alike(rng):
    d = setup_inputs(rng); d.update(lists(rng, "alike"))
    for k in ("tab",): d[k] = (d[k].astype(np.float32) * 1048576.0).astype(d[k].dtype)
    return d
def setup_inputs_distinct(rng):
    d = setup_inputs(rng); d.update(lists(rng, "distinct"))
    for k in ("tab",): d[k] = (d[k].astype(np.float32) * (1 / 1024.0)).astype(d[k].dtype)
    return d
def setup_inputs_edge(rng):
    d = setup_inputs(rng); d.update(lists(rng, "edge"))
    return d
def setup_inputs_hotrank(rng):
    d = setup_inputs(rng); d.update(lists(rng, "hotrank"))
    return d
def setup_inputs_own(rng):
    d = setup_inputs(rng); d.update(lists(rng, "own"))
    return d
def check_inputs(x):
    bad = []
    if x["idx"].min() < 0 or x["idx"].max() >= N * R: bad.append("idx out of range")
    return bad
def reference(tab, idx):
    A = np.concatenate(list(tab), axis=0)
    return {"y": np.stack([A[entries(idx[r])] for r in range(N)])}

@@ -1,0 +1,258 @@
+from concourse.bass import DstId, RemoteDMATransfer
+from concourse.mybir import AluOpType, ActivationFunctionType
+
+ZC = 4096
+PC = ZC + 1024
+LC = PC + 896
+
+SCRATCH = {
+    "lists": ("dram", [2048, 2], "int32"),
+    "xi": ("sbuf", [128, 32], "int32"),
+    "xr": ("sbuf", [128, 128], "float32"),
+    "ident": ("sbuf", [128, 128], "float32"),
+    "tabs": ("sbuf", [128, 2048], "float32"),
+    "win": ("sbuf", [128, LC], "float32"),
+    "vi": ("sbuf", [128, 128], "int32"),
+    "pos": ("sbuf", [128, 128], "int32"),
+    "ow": ("sbuf", [128, 64], "int32"),
+    "isme": ("sbuf", [128, 64], "int32"),
+    "dd": ("sbuf", [128, 64], "int32"),
+    "cst": ("sbuf", [128, 64], "int32"),
+    "pj": ("sbuf", [128, 64], "int32"),
+    "lam": ("sbuf", [128, 8], "int32"),
+    "offa": ("sbuf", [128, 64], "uint16"),
+    "offb": ("sbuf", [128, 64], "uint16"),
+    "g1": ("sbuf", [128, 1024], "float32"),
+    "g2": ("sbuf", [128, 896], "float32"),
+    "rr": ("sbuf", [128, 128], "float32"),
+    "yy": ("sbuf", [128, 128], "float32"),
+}
+for _b in range(8):
+    SCRATCH["ps%d" % _b] = ("psum", [128, 512], "float32")
+
+SEMAPHORES = (["ownl", "larr", "xl", "tl0", "tl1", "tl2", "tl3", "ones", "gi", "gid", "cs", "xrs", "pidx", "va",
+               "offas", "g1v", "g1s", "vb", "offbs", "parr", "g2v", "g2s", "aarr", "rrs", "pfin", "yys", "st0",
+               "st1", "lsem"] + ["pe%d" % i for i in range(8)] + ["ev%d" % i for i in range(8)])
+
+
+def rank_program(g, core, T, topo):
+    rank = T.rank_of(core)
+    if rank is None:
+        return
+    cores = list(T.cores)
+    n = len(cores)
+    chips = []
+    for c in cores:
+        if topo.chip(c) not in chips:
+            chips.append(topo.chip(c))
+    nch = len(chips)
+    chi = [chips.index(topo.chip(c)) for c in cores]
+    dlt = [topo.die(c) for c in cores]
+    assert nch == 8 and n == 16
+    for r in range(n):
+        assert chi[r] == r % nch
+    at = {}
+    for r in range(n):
+        at[(chi[r], dlt[r])] = r
+    assert len(at) == n
+    x, d = chi[rank], dlt[rank]
+    partner = at[(x, 1 - d)]
+    my = d * 64
+    ot = (1 - d) * 64
+
+    def slot_at(dst, src):
+        return dlt[src] * 8 + ((chi[src] - chi[dst] - 1) % nch)
+
+    def dst_id(r):
+        rid, pid, _ = topo.addr(cores[r])
+        return DstId(rid=rid, pnc=pid)
+
+    def bits(m):
+        return [1 << i for i in range(m.bit_length()) if (m >> i) & 1]
+
+    far = [r for r in range(n) if chi[r] != x]
+    far_mask = topo.mask(core, cores[partner])
+    for r in far:
+        assert topo.may_write(core, cores[r])
+        far_mask &= topo.mask(core, cores[r])
+    near_mask = topo.mask(core, cores[partner]) & ~far_mask
+    nfar, nnear = len(bits(far_mask)), len(bits(near_mask))
+
+    S = T.sem
+    tot = {}
+
+    def add(name, k):
+        tot[name] = tot.get(name, 0) + k
+
+    last = {}
+
+    def op(q, key, make, name):
+        if key in last:
+            q.wait_ge(S[last[key]], tot[last[key]])
+        make().then_inc(S[name], 1)
+        add(name, 1)
+        last[key] = name
+
+    V, A, P, Y = g.vector, g.scalar, g.tensor, g.sync
+    Copy = ActivationFunctionType.Copy
+
+    def vop(make, name):
+        op(V, "v", make, name)
+
+    def aop(make, name):
+        op(A, "a", make, name)
+
+    own = slot_at(rank, rank)
+    Y.dma_start(T.lists[own * 128:(own + 1) * 128, :], T.idx[:]).then_inc(S.ownl, 16)
+    add("ownl", 16)
+    for k in range(4):
+        q = Y if k % 2 == 0 else A
+        q.dma_start(T.tabs[:, k * 512:(k + 1) * 512], T.tab[k * 1024:(k + 1) * 1024, :]).then_inc(S["tl%d" % k], 16)
+        add("tl%d" % k, 16)
+
+    vop(lambda: V.memset(T.ident[:], 1.0), "ones")
+    g.iota(T.cst[:], [[16, 64]], ZC, 0).then_inc(S.gi, 1)
+    g.iota(T.pj[:], [[128, 64]], 0, 1).then_inc(S.gi, 1)
+    add("gi", 2)
+    g.wait_ge(S.ones, 1)
+    g.affine_select(T.ident[:], T.ident[:], [[-1, 128]], AluOpType.is_equal, 0.0, 0, 1).then_inc(S.gid, 1)
+    add("gid", 1)
+    V.wait_ge(S.gi, 2)
+    vop(lambda: V.tensor_scalar(out=T.pj[:], in0=T.pj[:], scalar1=15, scalar2=None, op0=AluOpType.bitwise_and), "cs")
+    vop(lambda: V.tensor_tensor(out=T.cst[:], in0=T.cst[:], in1=T.pj[:], op=AluOpType.add), "cs")
+
+    g.wait_ge(S.ownl, 16)
+    src = T.lists[own * 128:(own + 1) * 128, :]
+
+    def lslot(r):
+        k = slot_at(r, rank)
+        return T.lists[k * 128:(k + 1) * 128, :]
+
+    g.remote_dma_fused([
+        RemoteDMATransfer(dst_ids=[dst_id(r) for r in far], dma_engine_mask=far_mask, remote_sem=S.larr,
+                          srcs=[src], dsts=[lslot(r) for r in far]),
+        RemoteDMATransfer(dst_ids=[dst_id(partner)], dma_engine_mask=near_mask, remote_sem=S.larr,
+                          srcs=[src], dsts=[lslot(partner)]),
+    ], local_sem=S.lsem)
+    add("lsem", nfar + nnear)
+    add("larr", nfar * len(far) + nnear)
+    Y.wait_ge(S.ownl, 16)
+    Y.wait_ge(S.larr, tot["larr"])
+    Y.dma_start(T.xi[:], T.lists[:]).then_inc(S.xl, 16)
+    add("xl", 16)
+
+    bank = [0, 1, 2, 3, 4, 5, 0, 1]
+    P.wait_ge(S.gid, 1)
+
+    def turn_piece(i):
+        k, v = i // 2, i % 2
+        if v == 0:
+            P.wait_ge(S["tl%d" % k], 16)
+        if i >= 6:
+            P.wait_ge(S["ev%d" % (i - 6)], 4)
+        ps = T["ps%d" % bank[i]]
+        for m2 in range(2):
+            mu = v + 2 * m2
+            P.transpose(out=ps[:, m2:256:2], in_=T.tabs[:, k * 512 + mu * 128:k * 512 + (mu + 1) * 128],
+                        identity=T.ident[:]).then_inc(S["pe%d" % i], 1)
+            add("pe%d" % i, 1)
+
+    def evac_piece(i, vector):
+        k, v = i // 2, i % 2
+        ps = T["ps%d" % bank[i]]
+        (V if vector else A).wait_ge(S["pe%d" % i], 2)
+        for h in range(2):
+            for s in (h, 1 - h):
+                o = T.win[s * 64:(s + 1) * 64, k * 1024 + 2 * v + h:(k + 1) * 1024:4]
+                a = ps[h * 64:(h + 1) * 64, 0:256]
+                if vector:
+                    vop(lambda o=o, a=a: V.tensor_copy(out=o, in_=a), "ev%d" % i)
+                else:
+                    aop(lambda o=o, a=a: A.activation(out=o, in_=a, func=Copy), "ev%d" % i)
+
+    for i in range(7):
+        turn_piece(i)
+    P.wait_ge(S.xrs, 8)
+    P.transpose(out=T.ps6[:, 0:128], in_=T.xr[:], identity=T.ident[:]).then_inc(S.pidx, 1)
+    add("pidx", 1)
+    turn_piece(7)
+
+    by_vector = (0, 2, 4)
+    for i in by_vector:
+        evac_piece(i, True)
+    for i in range(8):
+        if i not in by_vector:
+            evac_piece(i, False)
+
+    V.wait_ge(S.xl, 16)
+    for gr in range(8):
+        vop(lambda gr=gr: V.tensor_copy(out=T.xr[:, gr * 16:(gr + 1) * 16], in_=T.xi[:, (gr // 4)::2]), "xrs")
+    V.wait_ge(S.pidx, 1)
+    vop(lambda: V.tensor_copy(out=T.vi[:], in_=T.ps6[:, 0:128]), "va")
+    vop(lambda: V.tensor_scalar(out=T.pos[:], in0=T.vi[:], scalar1=4095, scalar2=None,
+                                op0=AluOpType.bitwise_and), "va")
+    vop(lambda: V.tensor_copy(out=T.offa[:], in_=T.pos[:, ot:ot + 64]), "offas")
+
+    for i in range(8):
+        (A if i in by_vector else V).wait_ge(S["ev%d" % i], 4)
+    vop(lambda: V.tensor_copy(out=T.g1[:, 0:512], in_=T.win[:, 0:ZC].indirect(T.offa[:, 0:32])), "g1v")
+    A.wait_ge(S.offas, 1)
+    aop(lambda: A.activation(out=T.g1[:, 512:1024], in_=T.win[:, 0:ZC].indirect(T.offa[:, 32:64]), func=Copy), "g1s")
+    g.wait_ge(S.g1v, 1)
+    g.wait_ge(S.g1s, 1)
+    rid, pid, _ = topo.addr(cores[partner])
+    pm = topo.mask(core, cores[partner])
+    g.remote_dma(T.win[:, ZC:PC], T.g1[:], S.parr, S.lsem, pid, rid, pm)
+    add("lsem", len(bits(pm)))
+    add("parr", len(bits(pm)))
+
+    vop(lambda: V.tensor_scalar(out=T.ow[:], in0=T.vi[:, my:my + 64], scalar1=12, scalar2=None,
+                                op0=AluOpType.logical_shift_right), "vb")
+    vop(lambda: V.tensor_scalar(out=T.isme[:], in0=T.ow[:], scalar1=rank, scalar2=None,
+                                op0=AluOpType.is_equal), "vb")
+    vop(lambda: V.tensor_scalar(out=T.lam[:], in0=T.vi[:, my + 56:my + 64], scalar1=(nch - x) * 4096, scalar2=None,
+                                op0=AluOpType.add), "vb")
+    vop(lambda: V.tensor_scalar(out=T.lam[:], in0=T.lam[:], scalar1=12, scalar2=nch - 1,
+                                op0=AluOpType.logical_shift_right, op1=AluOpType.bitwise_and), "vb")
+    vop(lambda: V.tensor_scalar(out=T.lam[:], in0=T.lam[:], scalar1=128, scalar2=None, op0=AluOpType.mult), "vb")
+    vop(lambda: V.tensor_tensor(out=T.cst[:, 56:64], in0=T.cst[:, 56:64], in1=T.lam[:], op=AluOpType.add), "vb")
+    vop(lambda: V.tensor_tensor(out=T.dd[:], in0=T.pos[:, my:my + 64], in1=T.cst[:], op=AluOpType.subtract), "vb")
+    vop(lambda: V.tensor_tensor(out=T.dd[:], in0=T.dd[:], in1=T.isme[:], op=AluOpType.mult), "vb")
+    vop(lambda: V.tensor_tensor(out=T.dd[:], in0=T.dd[:], in1=T.cst[:], op=AluOpType.add), "vb")
+    vop(lambda: V.tensor_copy(out=T.offb[:], in_=T.dd[:]), "offbs")
+
+    V.wait_ge(S.parr, tot["parr"])
+    vop(lambda: V.tensor_copy(out=T.g2[:, 0:512], in_=T.win[:, 0:PC].indirect(T.offb[:, 0:32])), "g2v")
+    A.wait_ge(S.offbs, 1)
+    A.wait_ge(S.parr, tot["parr"])
+    aop(lambda: A.activation(out=T.g2[:, 512:896], in_=T.win[:, 0:PC].indirect(T.offb[:, 32:56]), func=Copy), "g2s")
+    g.wait_ge(S.g2v, 1)
+    g.wait_ge(S.g2s, 1)
+    eng = bits(far_mask)
+    trs = []
+    for q in range(nch - 1):
+        r = at[((x + 1 + q) % nch, d)]
+        lm = (x - chi[r]) % nch
+        c0 = PC + (lm - 1) * 128
+        trs.append(RemoteDMATransfer(dst_ids=[dst_id(r)], dma_engine_mask=eng[q], remote_sem=S.aarr,
+                                     src=T.g2[:, q * 128:(q + 1) * 128], dst=T.win[:, c0:c0 + 128]))
+    g.remote_dma_fused(trs, local_sem=S.lsem)
+    add("lsem", nch - 1)
+    add("aarr", nch - 1)
+
+    V.wait_ge(S.aarr, tot["aarr"])
+    vop(lambda: V.tensor_copy(out=T.rr[:], in_=T.win[:, 0:LC].indirect(T.offb[:, 56:64])), "rrs")
+    P.wait_ge(S.rrs, 1)
+    P.transpose(out=T.ps7[:, 0:128], in_=T.rr[:], identity=T.ident[:]).then_inc(S.pfin, 1)
+    add("pfin", 1)
+    V.wait_ge(S.pfin, 1)
+    vop(lambda: V.tensor_copy(out=T.yy[:], in_=T.ps7[:, 0:128]), "yys")
+    Y.wait_ge(S.yys, 1)
+    Y.dma_start(T.y[0:128, :], T.yy[:, 0:64]).then_inc(S.st0, 16)
+    add("st0", 16)
+    A.wait_ge(S.yys, 1)
+    A.dma_start(T.y[128:256, :], T.yy[:, 64:128]).then_inc(S.st1, 16)
+    add("st1", 16)
+
+    for name in SEMAPHORES:
+        g.wait_ge(S[name], tot[name])

@@ -1,9 +1,11 @@
 from concourse.bass import DstId, RemoteDMATransfer
 from concourse.mybir import AluOpType, ActivationFunctionType
 
+ND = 2
 ZC = 4096
-PC = ZC + 1024
-LC = PC + 896
+NP = 8 - ND
+PC = ZC + NP * 128
+LC = PC + (7 + ND) * 128
 
 SCRATCH = {
     "lists": ("dram", [2048, 2], "int32"),
@@ -20,19 +22,24 @@ SCRATCH = {
     "cst": ("sbuf", [128, 64], "int32"),
     "pj": ("sbuf", [128, 64], "int32"),
     "lam": ("sbuf", [128, 8], "int32"),
-    "offa": ("sbuf", [128, 64], "uint16"),
-    "offb": ("sbuf", [128, 64], "uint16"),
-    "g1": ("sbuf", [128, 1024], "float32"),
-    "g2": ("sbuf", [128, 896], "float32"),
+    "hi": ("sbuf", [128, 8], "int32"),
+    "ge": ("sbuf", [128, 8], "int32"),
+    "offp": ("sbuf", [128, 128], "uint16"),
+    "offb": ("sbuf", [128, 56], "uint16"),
+    "offm": ("sbuf", [128, 8], "uint16"),
+    "g1": ("sbuf", [128, NP * 128], "float32"),
+    "gd": ("sbuf", [128, 2 * ND * 128], "float32"),
+    "g2": ("sbuf", [128, (NP - 1) * 128], "float32"),
     "rr": ("sbuf", [128, 128], "float32"),
     "yy": ("sbuf", [128, 128], "float32"),
 }
 for _b in range(8):
     SCRATCH["ps%d" % _b] = ("psum", [128, 512], "float32")
 
-SEMAPHORES = (["ownl", "larr", "xl", "tl0", "tl1", "tl2", "tl3", "ones", "gi", "gid", "cs", "xrs", "pidx", "va",
-               "offas", "g1v", "g1s", "vb", "offbs", "parr", "g2v", "g2s", "aarr", "rrs", "pfin", "yys", "st0",
-               "st1", "lsem"] + ["pe%d" % i for i in range(8)] + ["ev%d" % i for i in range(8)])
+SEMAPHORES = (["ownl", "larr", "xl", "ones", "gi", "gid", "cs", "xrs", "pidx", "va", "offps", "vb", "offbs", "aarr",
+               "rrs", "pfin", "yys", "st0", "st1", "lsem", "g1v", "g1s", "gdv", "gds", "g2v", "g2s", "g2c", "vm",
+               "parr"]
+              + ["tl%d" % i for i in range(8)] + ["pe%d" % i for i in range(9)] + ["ev%d" % i for i in range(9)])
 
 
 def rank_program(g, core, T, topo):
@@ -49,13 +56,14 @@ def rank_program(g, core, T, topo):
     chi = [chips.index(topo.chip(c)) for c in cores]
     dlt = [topo.die(c) for c in cores]
     assert nch == 8 and n == 16
-    for r in range(n):
-        assert chi[r] == r % nch
     at = {}
     for r in range(n):
         at[(chi[r], dlt[r])] = r
     assert len(at) == n
     x, d = chi[rank], dlt[rank]
+    for r in range(n):
+        assert chi[r] == r % nch
+        assert (dlt[r] == d) == (r // nch == rank // nch)
     partner = at[(x, 1 - d)]
     my = d * 64
     ot = (1 - d) * 64
@@ -102,16 +110,22 @@ def rank_program(g, core, T, topo):
     def aop(make, name):
         op(A, "a", make, name)
 
+    def vpick(out, win_end, off, name):
+        vop(lambda: V.tensor_copy(out=out, in_=T.win[:, 0:win_end].indirect(off)), name)
+
+    def apick(out, win_end, off, name):
+        aop(lambda: A.activation(out=out, in_=T.win[:, 0:win_end].indirect(off), func=Copy), name)
+
     own = slot_at(rank, rank)
     Y.dma_start(T.lists[own * 128:(own + 1) * 128, :], T.idx[:]).then_inc(S.ownl, 16)
     add("ownl", 16)
-    for k in range(4):
+    for k in range(8):
         q = Y if k % 2 == 0 else A
-        q.dma_start(T.tabs[:, k * 512:(k + 1) * 512], T.tab[k * 1024:(k + 1) * 1024, :]).then_inc(S["tl%d" % k], 16)
+        q.dma_start(T.tabs[:, k * 256:(k + 1) * 256], T.tab[k * 512:(k + 1) * 512, :]).then_inc(S["tl%d" % k], 16)
         add("tl%d" % k, 16)
 
     vop(lambda: V.memset(T.ident[:], 1.0), "ones")
-    g.iota(T.cst[:], [[16, 64]], ZC, 0).then_inc(S.gi, 1)
+    g.iota(T.cst[:], [[16, 64]], ZC - ND * 128, 0).then_inc(S.gi, 1)
     g.iota(T.pj[:], [[128, 64]], 0, 1).then_inc(S.gi, 1)
     add("gi", 2)
     g.wait_ge(S.ones, 1)
@@ -141,48 +155,52 @@ def rank_program(g, core, T, topo):
     Y.dma_start(T.xi[:], T.lists[:]).then_inc(S.xl, 16)
     add("xl", 16)
 
-    bank = [0, 1, 2, 3, 4, 5, 0, 1]
+    bank = [0, 1, 2, 3, 4, 5, 0, 1, 2]
     P.wait_ge(S.gid, 1)
 
-    def turn_piece(i):
-        k, v = i // 2, i % 2
-        if v == 0:
+    def turn_unit(i):
+        k = min(i, 7)
+        if i < 8:
             P.wait_ge(S["tl%d" % k], 16)
         if i >= 6:
             P.wait_ge(S["ev%d" % (i - 6)], 4)
         ps = T["ps%d" % bank[i]]
-        for m2 in range(2):
-            mu = v + 2 * m2
-            P.transpose(out=ps[:, m2:256:2], in_=T.tabs[:, k * 512 + mu * 128:k * 512 + (mu + 1) * 128],
+        for m2 in ((0, 1) if i < 7 else (i - 7,)):
+            o = ps[:, m2:256:2] if i < 7 else ps[:, 0:128]
+            P.transpose(out=o, in_=T.tabs[:, k * 256 + m2 * 128:k * 256 + (m2 + 1) * 128],
                         identity=T.ident[:]).then_inc(S["pe%d" % i], 1)
             add("pe%d" % i, 1)
 
-    def evac_piece(i, vector):
-        k, v = i // 2, i % 2
+    def evac_unit(i, vector):
+        k = min(i, 7)
         ps = T["ps%d" % bank[i]]
-        (V if vector else A).wait_ge(S["pe%d" % i], 2)
+        (V if vector else A).wait_ge(S["pe%d" % i], tot["pe%d" % i])
         for h in range(2):
             for s in (h, 1 - h):
-                o = T.win[s * 64:(s + 1) * 64, k * 1024 + 2 * v + h:(k + 1) * 1024:4]
-                a = ps[h * 64:(h + 1) * 64, 0:256]
+                if i < 7:
+                    o = T.win[s * 64:(s + 1) * 64, k * 512 + h:(k + 1) * 512:2]
+                    a = ps[h * 64:(h + 1) * 64, 0:256]
+                else:
+                    o = T.win[s * 64:(s + 1) * 64, k * 512 + 2 * (i - 7) + h:(k + 1) * 512:4]
+                    a = ps[h * 64:(h + 1) * 64, 0:128]
                 if vector:
                     vop(lambda o=o, a=a: V.tensor_copy(out=o, in_=a), "ev%d" % i)
                 else:
                     aop(lambda o=o, a=a: A.activation(out=o, in_=a, func=Copy), "ev%d" % i)
 
-    for i in range(7):
-        turn_piece(i)
+    for i in range(8):
+        turn_unit(i)
     P.wait_ge(S.xrs, 8)
     P.transpose(out=T.ps6[:, 0:128], in_=T.xr[:], identity=T.ident[:]).then_inc(S.pidx, 1)
     add("pidx", 1)
-    turn_piece(7)
+    turn_unit(8)
 
-    by_vector = (0, 2, 4)
-    for i in by_vector:
-        evac_piece(i, True)
-    for i in range(8):
+    by_vector = (0, 2, 4, 8)
+    for i in (0, 2, 4):
+        evac_unit(i, True)
+    for i in range(9):
         if i not in by_vector:
-            evac_piece(i, False)
+            evac_unit(i, False)
 
     V.wait_ge(S.xl, 16)
     for gr in range(8):
@@ -191,13 +209,16 @@ def rank_program(g, core, T, topo):
     vop(lambda: V.tensor_copy(out=T.vi[:], in_=T.ps6[:, 0:128]), "va")
     vop(lambda: V.tensor_scalar(out=T.pos[:], in0=T.vi[:], scalar1=4095, scalar2=None,
                                 op0=AluOpType.bitwise_and), "va")
-    vop(lambda: V.tensor_copy(out=T.offa[:], in_=T.pos[:, ot:ot + 64]), "offas")
-
-    for i in range(8):
+    vop(lambda: V.tensor_copy(out=T.offp[:], in_=T.pos[:]), "offps")
+    evac_unit(8, True)
+    for i in range(9):
         (A if i in by_vector else V).wait_ge(S["ev%d" % i], 4)
-    vop(lambda: V.tensor_copy(out=T.g1[:, 0:512], in_=T.win[:, 0:ZC].indirect(T.offa[:, 0:32])), "g1v")
-    A.wait_ge(S.offas, 1)
-    aop(lambda: A.activation(out=T.g1[:, 512:1024], in_=T.win[:, 0:ZC].indirect(T.offa[:, 32:64]), func=Copy), "g1s")
+    A.wait_ge(S.offps, 1)
+
+    c1 = ot + ND * 8
+    hc = NP * 4
+    vpick(T.g1[:, 0:hc * 16], ZC, T.offp[:, c1:c1 + hc], "g1v")
+    apick(T.g1[:, hc * 16:NP * 128], ZC, T.offp[:, c1 + hc:ot + 64], "g1s")
     g.wait_ge(S.g1v, 1)
     g.wait_ge(S.g1s, 1)
     rid, pid, _ = topo.addr(cores[partner])
@@ -206,42 +227,76 @@ def rank_program(g, core, T, topo):
     add("lsem", len(bits(pm)))
     add("parr", len(bits(pm)))
 
+    vpick(T.gd[:, 0:ND * 128], ZC, T.offp[:, my:my + ND * 8], "gdv")
+    apick(T.gd[:, ND * 128:2 * ND * 128], ZC, T.offp[:, ot:ot + ND * 8], "gds")
+    g.wait_ge(S.gdv, 1)
+    g.wait_ge(S.gds, 1)
+    eng = bits(far_mask)
+    pair = [eng[2 * j] | eng[2 * j + 1] for j in range(len(eng) // 2)]
+
+    def answer(r, first_slot, src_ap, mask):
+        lm = (x - chi[r]) % nch
+        c0 = ZC + (first_slot + lm) * 128
+        k = len(bits(mask))
+        add("lsem", k)
+        add("aarr", k)
+        return RemoteDMATransfer(dst_ids=[dst_id(r)], dma_engine_mask=mask, remote_sem=S.aarr, src=src_ap,
+                                 dst=T.win[:, c0:c0 + 128])
+
+    trs = []
+    for q in range(ND):
+        ch = (x + 1 + q) % nch
+        trs.append(answer(at[(ch, d)], NP - 1, T.gd[:, q * 128:(q + 1) * 128], pair[2 * q]))
+        trs.append(answer(at[(ch, 1 - d)], NP - 1 + ND, T.gd[:, (ND + q) * 128:(ND + q + 1) * 128], pair[2 * q + 1]))
+    g.remote_dma_fused(trs, local_sem=S.lsem)
+
+    m6 = 56
     vop(lambda: V.tensor_scalar(out=T.ow[:], in0=T.vi[:, my:my + 64], scalar1=12, scalar2=None,
                                 op0=AluOpType.logical_shift_right), "vb")
     vop(lambda: V.tensor_scalar(out=T.isme[:], in0=T.ow[:], scalar1=rank, scalar2=None,
                                 op0=AluOpType.is_equal), "vb")
-    vop(lambda: V.tensor_scalar(out=T.lam[:], in0=T.vi[:, my + 56:my + 64], scalar1=(nch - x) * 4096, scalar2=None,
-                                op0=AluOpType.add), "vb")
-    vop(lambda: V.tensor_scalar(out=T.lam[:], in0=T.lam[:], scalar1=12, scalar2=nch - 1,
-                                op0=AluOpType.logical_shift_right, op1=AluOpType.bitwise_and), "vb")
-    vop(lambda: V.tensor_scalar(out=T.lam[:], in0=T.lam[:], scalar1=128, scalar2=None, op0=AluOpType.mult), "vb")
-    vop(lambda: V.tensor_tensor(out=T.cst[:, 56:64], in0=T.cst[:, 56:64], in1=T.lam[:], op=AluOpType.add), "vb")
-    vop(lambda: V.tensor_tensor(out=T.dd[:], in0=T.pos[:, my:my + 64], in1=T.cst[:], op=AluOpType.subtract), "vb")
-    vop(lambda: V.tensor_tensor(out=T.dd[:], in0=T.dd[:], in1=T.isme[:], op=AluOpType.mult), "vb")
-    vop(lambda: V.tensor_tensor(out=T.dd[:], in0=T.dd[:], in1=T.cst[:], op=AluOpType.add), "vb")
-    vop(lambda: V.tensor_copy(out=T.offb[:], in_=T.dd[:]), "offbs")
+    vop(lambda: V.tensor_tensor(out=T.dd[:, 0:m6], in0=T.pos[:, my:my + m6], in1=T.cst[:, 0:m6],
+                                op=AluOpType.subtract), "vb")
+    vop(lambda: V.tensor_tensor(out=T.dd[:, 0:m6], in0=T.dd[:, 0:m6], in1=T.isme[:, 0:m6], op=AluOpType.mult), "vb")
+    vop(lambda: V.tensor_tensor(out=T.dd[:, 0:m6], in0=T.dd[:, 0:m6], in1=T.cst[:, 0:m6], op=AluOpType.add), "vb")
+    vop(lambda: V.tensor_copy(out=T.offb[:], in_=T.dd[:, 0:m6]), "offbs")
 
+    o0 = ND * 8
     V.wait_ge(S.parr, tot["parr"])
-    vop(lambda: V.tensor_copy(out=T.g2[:, 0:512], in_=T.win[:, 0:PC].indirect(T.offb[:, 0:32])), "g2v")
+    vpick(T.g2[:, 0:256], PC, T.offb[:, o0:o0 + 16], "g2v")
     A.wait_ge(S.offbs, 1)
     A.wait_ge(S.parr, tot["parr"])
-    aop(lambda: A.activation(out=T.g2[:, 512:896], in_=T.win[:, 0:PC].indirect(T.offb[:, 32:56]), func=Copy), "g2s")
+    apick(T.g2[:, 256:512], PC, T.offb[:, o0 + 16:o0 + 32], "g2s")
+    apick(T.g2[:, 512:640], PC, T.offb[:, o0 + 32:o0 + 40], "g2c")
     g.wait_ge(S.g2v, 1)
     g.wait_ge(S.g2s, 1)
-    eng = bits(far_mask)
-    trs = []
-    for q in range(nch - 1):
-        r = at[((x + 1 + q) % nch, d)]
-        lm = (x - chi[r]) % nch
-        c0 = PC + (lm - 1) * 128
-        trs.append(RemoteDMATransfer(dst_ids=[dst_id(r)], dma_engine_mask=eng[q], remote_sem=S.aarr,
-                                     src=T.g2[:, q * 128:(q + 1) * 128], dst=T.win[:, c0:c0 + 128]))
-    g.remote_dma_fused(trs, local_sem=S.lsem)
-    add("lsem", nch - 1)
-    add("aarr", nch - 1)
+    g.remote_dma_fused([answer(at[((x + 1 + ND + j) % nch, d)], NP - 1, T.g2[:, j * 128:(j + 1) * 128], pair[j])
+                        for j in range(4)], local_sem=S.lsem)
+    g.wait_ge(S.g2c, 1)
+    g.remote_dma_fused([answer(at[((x + 1 + ND + 4) % nch, d)], NP - 1, T.g2[:, 512:640], far_mask)], local_sem=S.lsem)
+
+    me8 = slice(my + 56, my + 64)
+    vop(lambda: V.tensor_scalar(out=T.lam[:], in0=T.vi[:, me8], scalar1=(nch - x) * 4096, scalar2=None,
+                                op0=AluOpType.add), "vm")
+    vop(lambda: V.tensor_scalar(out=T.lam[:], in0=T.lam[:], scalar1=12, scalar2=nch - 1,
+                                op0=AluOpType.logical_shift_right, op1=AluOpType.bitwise_and), "vm")
+    vop(lambda: V.tensor_scalar(out=T.hi[:], in0=T.vi[:, me8], scalar1=15, scalar2=None,
+                                op0=AluOpType.logical_shift_right), "vm")
+    vop(lambda: V.tensor_scalar(out=T.hi[:], in0=T.hi[:], scalar1=rank // nch, scalar2=ND,
+                                op0=AluOpType.not_equal, op1=AluOpType.mult), "vm")
+    vop(lambda: V.tensor_scalar(out=T.ge[:], in0=T.lam[:], scalar1=nch - ND, scalar2=None,
+                                op0=AluOpType.is_ge), "vm")
+    vop(lambda: V.tensor_tensor(out=T.ge[:], in0=T.ge[:], in1=T.hi[:], op=AluOpType.mult), "vm")
+    vop(lambda: V.tensor_tensor(out=T.lam[:], in0=T.lam[:], in1=T.ge[:], op=AluOpType.add), "vm")
+    vop(lambda: V.tensor_scalar(out=T.lam[:], in0=T.lam[:], scalar1=128, scalar2=None, op0=AluOpType.mult), "vm")
+    vop(lambda: V.tensor_tensor(out=T.lam[:], in0=T.lam[:], in1=T.cst[:, 56:64], op=AluOpType.add), "vm")
+    vop(lambda: V.tensor_tensor(out=T.hi[:], in0=T.pos[:, me8], in1=T.lam[:], op=AluOpType.subtract), "vm")
+    vop(lambda: V.tensor_tensor(out=T.hi[:], in0=T.hi[:], in1=T.isme[:, 56:64], op=AluOpType.mult), "vm")
+    vop(lambda: V.tensor_tensor(out=T.hi[:], in0=T.hi[:], in1=T.lam[:], op=AluOpType.add), "vm")
+    vop(lambda: V.tensor_copy(out=T.offm[:], in_=T.hi[:]), "vm")
 
     V.wait_ge(S.aarr, tot["aarr"])
-    vop(lambda: V.tensor_copy(out=T.rr[:], in_=T.win[:, 0:LC].indirect(T.offb[:, 56:64])), "rrs")
+    vpick(T.rr[:], LC, T.offm[:], "rrs")
     P.wait_ge(S.rrs, 1)
     P.transpose(out=T.ps7[:, 0:128], in_=T.rr[:], identity=T.ident[:]).then_inc(S.pfin, 1)
     add("pfin", 1)

@@ -37,7 +37,7 @@ for _b in range(8):
     SCRATCH["ps%d" % _b] = ("psum", [128, 512], "float32")
 
 SEMAPHORES = (["ownl", "larr", "xl", "ones", "gi", "gid", "cs", "xrs", "pidx", "va", "offps", "vb", "offbs", "aarr",
-               "rrs", "pfin", "yys", "st0", "st1", "lsem", "g1v", "g1s", "gdv", "gds", "g2v", "g2s", "g2c", "vm",
+               "rrs", "pfin", "yys", "st0", "st1", "lsem", "g1v", "g1s", "gds", "g2v", "g2s", "g2c", "vm",
                "parr"]
               + ["tl%d" % i for i in range(8)] + ["pe%d" % i for i in range(9)] + ["ev%d" % i for i in range(9)])
 
@@ -94,8 +94,8 @@ def rank_program(g, core, T, topo):
 
     last = {}
 
-    def op(q, key, make, name):
-        if key in last:
+    def op(q, key, make, name, free=False):
+        if key in last and not free:
             q.wait_ge(S[last[key]], tot[last[key]])
         make().then_inc(S[name], 1)
         add(name, 1)
@@ -104,11 +104,11 @@ def rank_program(g, core, T, topo):
     V, A, P, Y = g.vector, g.scalar, g.tensor, g.sync
     Copy = ActivationFunctionType.Copy
 
-    def vop(make, name):
-        op(V, "v", make, name)
+    def vop(make, name, free=False):
+        op(V, "v", make, name, free)
 
-    def aop(make, name):
-        op(A, "a", make, name)
+    def aop(make, name, free=False):
+        op(A, "a", make, name, free)
 
     def vpick(out, win_end, off, name):
         vop(lambda: V.tensor_copy(out=out, in_=T.win[:, 0:win_end].indirect(off)), name)
@@ -177,6 +177,7 @@ def rank_program(g, core, T, topo):
         (V if vector else A).wait_ge(S["pe%d" % i], tot["pe%d" % i])
         for h in range(2):
             for s in (h, 1 - h):
+                fr = (h, s) != (0, 0)
                 if i < 7:
                     o = T.win[s * 64:(s + 1) * 64, k * 512 + h:(k + 1) * 512:2]
                     a = ps[h * 64:(h + 1) * 64, 0:256]
@@ -184,9 +185,9 @@ def rank_program(g, core, T, topo):
                     o = T.win[s * 64:(s + 1) * 64, k * 512 + 2 * (i - 7) + h:(k + 1) * 512:4]
                     a = ps[h * 64:(h + 1) * 64, 0:128]
                 if vector:
-                    vop(lambda o=o, a=a: V.tensor_copy(out=o, in_=a), "ev%d" % i)
+                    vop(lambda o=o, a=a: V.tensor_copy(out=o, in_=a), "ev%d" % i, fr)
                 else:
-                    aop(lambda o=o, a=a: A.activation(out=o, in_=a, func=Copy), "ev%d" % i)
+                    aop(lambda o=o, a=a: A.activation(out=o, in_=a, func=Copy), "ev%d" % i, fr)
 
     for i in range(8):
         turn_unit(i)
@@ -204,7 +205,8 @@ def rank_program(g, core, T, topo):
 
     V.wait_ge(S.xl, 16)
     for gr in range(8):
-        vop(lambda gr=gr: V.tensor_copy(out=T.xr[:, gr * 16:(gr + 1) * 16], in_=T.xi[:, (gr // 4)::2]), "xrs")
+        vop(lambda gr=gr: V.tensor_copy(out=T.xr[:, gr * 16:(gr + 1) * 16], in_=T.xi[:, (gr // 4)::2]), "xrs",
+            gr > 0)
     V.wait_ge(S.pidx, 1)
     vop(lambda: V.tensor_copy(out=T.vi[:], in_=T.ps6[:, 0:128]), "va")
     vop(lambda: V.tensor_scalar(out=T.pos[:], in0=T.vi[:], scalar1=4095, scalar2=None,
@@ -227,10 +229,9 @@ def rank_program(g, core, T, topo):
     add("lsem", len(bits(pm)))
     add("parr", len(bits(pm)))
 
-    vpick(T.gd[:, 0:ND * 128], ZC, T.offp[:, my:my + ND * 8], "gdv")
+    apick(T.gd[:, 0:ND * 128], ZC, T.offp[:, my:my + ND * 8], "gds")
     apick(T.gd[:, ND * 128:2 * ND * 128], ZC, T.offp[:, ot:ot + ND * 8], "gds")
-    g.wait_ge(S.gdv, 1)
-    g.wait_ge(S.gds, 1)
+    g.wait_ge(S.gds, 2)
     eng = bits(far_mask)
     pair = [eng[2 * j] | eng[2 * j + 1] for j in range(len(eng) // 2)]
 

@@ -4,8 +4,11 @@ from concourse.mybir import AluOpType, ActivationFunctionType
 ND = 2
 ZC = 4096
 NP = 8 - ND
+NA = 4
+AC = ZC + NA * 128
 PC = ZC + NP * 128
 LC = PC + (7 + ND) * 128
+BIG = 16384
 
 SCRATCH = {
     "lists": ("dram", [2048, 2], "int32"),
@@ -17,8 +20,9 @@ SCRATCH = {
     "vi": ("sbuf", [128, 128], "int32"),
     "pos": ("sbuf", [128, 128], "int32"),
     "ow": ("sbuf", [128, 64], "int32"),
-    "isme": ("sbuf", [128, 64], "int32"),
+    "notme": ("sbuf", [128, 64], "int32"),
     "dd": ("sbuf", [128, 64], "int32"),
+    "mn": ("sbuf", [128, 64], "int32"),
     "cst": ("sbuf", [128, 64], "int32"),
     "pj": ("sbuf", [128, 64], "int32"),
     "lam": ("sbuf", [128, 8], "int32"),
@@ -37,8 +41,8 @@ for _b in range(8):
     SCRATCH["ps%d" % _b] = ("psum", [128, 512], "float32")
 
 SEMAPHORES = (["ownl", "larr", "xl", "ones", "gi", "gid", "cs", "xrs", "pidx", "va", "offps", "vb", "offbs", "aarr",
-               "rrs", "pfin", "yys", "st0", "st1", "lsem", "g1v", "g1s", "gds", "g2v", "g2s", "g2c", "vm",
-               "parr"]
+               "rrs", "pfin", "yys", "st0", "st1", "lsem", "g1v", "g1s", "g1bs", "gdv", "gds", "g2v", "g2s", "g2c",
+               "vm", "parr", "parb"]
               + ["tl%d" % i for i in range(8)] + ["pe%d" % i for i in range(9)] + ["ev%d" % i for i in range(9)])
 
 
@@ -110,11 +114,11 @@ def rank_program(g, core, T, topo):
     def aop(make, name, free=False):
         op(A, "a", make, name, free)
 
-    def vpick(out, win_end, off, name):
-        vop(lambda: V.tensor_copy(out=out, in_=T.win[:, 0:win_end].indirect(off)), name)
+    def vpick(out, win_end, off, name, free=False):
+        vop(lambda: V.tensor_copy(out=out, in_=T.win[:, 0:win_end].indirect(off)), name, free)
 
-    def apick(out, win_end, off, name):
-        aop(lambda: A.activation(out=out, in_=T.win[:, 0:win_end].indirect(off), func=Copy), name)
+    def apick(out, win_end, off, name, free=False):
+        aop(lambda: A.activation(out=out, in_=T.win[:, 0:win_end].indirect(off), func=Copy), name, free)
 
     own = slot_at(rank, rank)
     Y.dma_start(T.lists[own * 128:(own + 1) * 128, :], T.idx[:]).then_inc(S.ownl, 16)
@@ -218,20 +222,23 @@ def rank_program(g, core, T, topo):
     A.wait_ge(S.offps, 1)
 
     c1 = ot + ND * 8
-    hc = NP * 4
-    vpick(T.g1[:, 0:hc * 16], ZC, T.offp[:, c1:c1 + hc], "g1v")
-    apick(T.g1[:, hc * 16:NP * 128], ZC, T.offp[:, c1 + hc:ot + 64], "g1s")
+    ha = NA * 4
+    cb = c1 + NA * 8
+    vpick(T.g1[:, 0:ha * 16], ZC, T.offp[:, c1:c1 + ha], "g1v")
+    apick(T.g1[:, ha * 16:NA * 128], ZC, T.offp[:, c1 + ha:cb], "g1s")
+    vpick(T.gd[:, 0:ND * 128], ZC, T.offp[:, my:my + ND * 8], "gdv", True)
+    apick(T.gd[:, ND * 128:2 * ND * 128], ZC, T.offp[:, ot:ot + ND * 8], "gds", True)
+    apick(T.g1[:, NA * 128:NP * 128], ZC, T.offp[:, cb:ot + 64], "g1bs", True)
+
+    rid, pid, _ = topo.addr(cores[partner])
     g.wait_ge(S.g1v, 1)
     g.wait_ge(S.g1s, 1)
-    rid, pid, _ = topo.addr(cores[partner])
-    pm = topo.mask(core, cores[partner])
-    g.remote_dma(T.win[:, ZC:PC], T.g1[:], S.parr, S.lsem, pid, rid, pm)
-    add("lsem", len(bits(pm)))
-    add("parr", len(bits(pm)))
+    g.remote_dma(T.win[:, ZC:AC], T.g1[:, 0:NA * 128], S.parr, S.lsem, pid, rid, near_mask)
+    add("lsem", nnear)
+    add("parr", nnear)
 
-    apick(T.gd[:, 0:ND * 128], ZC, T.offp[:, my:my + ND * 8], "gds")
-    apick(T.gd[:, ND * 128:2 * ND * 128], ZC, T.offp[:, ot:ot + ND * 8], "gds")
-    g.wait_ge(S.gds, 2)
+    g.wait_ge(S.gdv, 1)
+    g.wait_ge(S.gds, 1)
     eng = bits(far_mask)
     pair = [eng[2 * j] | eng[2 * j + 1] for j in range(len(eng) // 2)]
 
@@ -251,24 +258,28 @@ def rank_program(g, core, T, topo):
         trs.append(answer(at[(ch, 1 - d)], NP - 1 + ND, T.gd[:, (ND + q) * 128:(ND + q + 1) * 128], pair[2 * q + 1]))
     g.remote_dma_fused(trs, local_sem=S.lsem)
 
+    g.wait_ge(S.g1bs, 1)
+    g.remote_dma(T.win[:, AC:PC], T.g1[:, NA * 128:NP * 128], S.parb, S.lsem, pid, rid, near_mask)
+    add("lsem", nnear)
+    add("parb", nnear)
+
     m6 = 56
     vop(lambda: V.tensor_scalar(out=T.ow[:], in0=T.vi[:, my:my + 64], scalar1=12, scalar2=None,
-                                op0=AluOpType.logical_shift_right), "vb")
-    vop(lambda: V.tensor_scalar(out=T.isme[:], in0=T.ow[:], scalar1=rank, scalar2=None,
-                                op0=AluOpType.is_equal), "vb")
-    vop(lambda: V.tensor_tensor(out=T.dd[:, 0:m6], in0=T.pos[:, my:my + m6], in1=T.cst[:, 0:m6],
-                                op=AluOpType.subtract), "vb")
-    vop(lambda: V.tensor_tensor(out=T.dd[:, 0:m6], in0=T.dd[:, 0:m6], in1=T.isme[:, 0:m6], op=AluOpType.mult), "vb")
-    vop(lambda: V.tensor_tensor(out=T.dd[:, 0:m6], in0=T.dd[:, 0:m6], in1=T.cst[:, 0:m6], op=AluOpType.add), "vb")
-    vop(lambda: V.tensor_copy(out=T.offb[:], in_=T.dd[:, 0:m6]), "offbs")
+                                op0=AluOpType.logical_shift_right), "vb", True)
+    vop(lambda: V.tensor_scalar(out=T.notme[:], in0=T.ow[:], scalar1=rank, scalar2=BIG,
+                                op0=AluOpType.not_equal, op1=AluOpType.mult), "vb")
+    vop(lambda: V.tensor_tensor(out=T.dd[:], in0=T.notme[:], in1=T.pos[:, my:my + 64], op=AluOpType.add), "vb")
+    vop(lambda: V.tensor_tensor(out=T.mn[:, 0:m6], in0=T.dd[:, 0:m6], in1=T.cst[:, 0:m6], op=AluOpType.min), "vb")
+    vop(lambda: V.tensor_copy(out=T.offb[:], in_=T.mn[:, 0:m6]), "offbs")
 
     o0 = ND * 8
     V.wait_ge(S.parr, tot["parr"])
-    vpick(T.g2[:, 0:256], PC, T.offb[:, o0:o0 + 16], "g2v")
+    vpick(T.g2[:, 0:256], AC, T.offb[:, o0:o0 + 16], "g2v")
     A.wait_ge(S.offbs, 1)
     A.wait_ge(S.parr, tot["parr"])
-    apick(T.g2[:, 256:512], PC, T.offb[:, o0 + 16:o0 + 32], "g2s")
-    apick(T.g2[:, 512:640], PC, T.offb[:, o0 + 32:o0 + 40], "g2c")
+    apick(T.g2[:, 256:512], AC, T.offb[:, o0 + 16:o0 + 32], "g2s", True)
+    A.wait_ge(S.parb, tot["parb"])
+    apick(T.g2[:, 512:640], PC, T.offb[:, o0 + 32:o0 + 40], "g2c", True)
     g.wait_ge(S.g2v, 1)
     g.wait_ge(S.g2s, 1)
     g.remote_dma_fused([answer(at[((x + 1 + ND + j) % nch, d)], NP - 1, T.g2[:, j * 128:(j + 1) * 128], pair[j])
@@ -291,11 +302,10 @@ def rank_program(g, core, T, topo):
     vop(lambda: V.tensor_tensor(out=T.lam[:], in0=T.lam[:], in1=T.ge[:], op=AluOpType.add), "vm")
     vop(lambda: V.tensor_scalar(out=T.lam[:], in0=T.lam[:], scalar1=128, scalar2=None, op0=AluOpType.mult), "vm")
     vop(lambda: V.tensor_tensor(out=T.lam[:], in0=T.lam[:], in1=T.cst[:, 56:64], op=AluOpType.add), "vm")
-    vop(lambda: V.tensor_tensor(out=T.hi[:], in0=T.pos[:, me8], in1=T.lam[:], op=AluOpType.subtract), "vm")
-    vop(lambda: V.tensor_tensor(out=T.hi[:], in0=T.hi[:], in1=T.isme[:, 56:64], op=AluOpType.mult), "vm")
-    vop(lambda: V.tensor_tensor(out=T.hi[:], in0=T.hi[:], in1=T.lam[:], op=AluOpType.add), "vm")
+    vop(lambda: V.tensor_tensor(out=T.hi[:], in0=T.dd[:, 56:64], in1=T.lam[:], op=AluOpType.min), "vm")
     vop(lambda: V.tensor_copy(out=T.offm[:], in_=T.hi[:]), "vm")
 
+    V.wait_ge(S.parb, tot["parb"])
     V.wait_ge(S.aarr, tot["aarr"])
     vpick(T.rr[:], LC, T.offm[:], "rrs")
     P.wait_ge(S.rrs, 1)

from concourse.bass import DstId, RemoteDMATransfer
from concourse.mybir import AluOpType, ActivationFunctionType

ND = 2
ZC = 4096
NP = 8 - ND
NA = 4
AC = ZC + NA * 128
PC = ZC + NP * 128
LC = PC + (7 + ND) * 128
BIG = 16384

SCRATCH = {
    "lists": ("dram", [2048, 2], "int32"),
    "xi": ("sbuf", [128, 32], "int32"),
    "xr": ("sbuf", [128, 128], "float32"),
    "ident": ("sbuf", [128, 128], "float32"),
    "tabs": ("sbuf", [128, 2048], "float32"),
    "win": ("sbuf", [128, LC], "float32"),
    "vi": ("sbuf", [128, 128], "int32"),
    "pos": ("sbuf", [128, 128], "int32"),
    "ow": ("sbuf", [128, 64], "int32"),
    "notme": ("sbuf", [128, 64], "int32"),
    "dd": ("sbuf", [128, 64], "int32"),
    "mn": ("sbuf", [128, 64], "int32"),
    "cst": ("sbuf", [128, 64], "int32"),
    "pj": ("sbuf", [128, 64], "int32"),
    "lam": ("sbuf", [128, 8], "int32"),
    "hi": ("sbuf", [128, 8], "int32"),
    "ge": ("sbuf", [128, 8], "int32"),
    "offp": ("sbuf", [128, 128], "uint16"),
    "offb": ("sbuf", [128, 56], "uint16"),
    "offm": ("sbuf", [128, 8], "uint16"),
    "g1": ("sbuf", [128, NP * 128], "float32"),
    "gd": ("sbuf", [128, 2 * ND * 128], "float32"),
    "g2": ("sbuf", [128, (NP - 1) * 128], "float32"),
    "rr": ("sbuf", [128, 128], "float32"),
    "yy": ("sbuf", [128, 128], "float32"),
}
for _b in range(8):
    SCRATCH["ps%d" % _b] = ("psum", [128, 512], "float32")

SEMAPHORES = (["ownl", "larr", "xl", "ones", "gi", "gid", "cs", "xrs", "pidx", "va", "offps", "vb", "offbs", "aarr",
               "rrs", "pfin", "yys", "st0", "st1", "lsem", "g1v", "g1s", "g1bs", "gdv", "gds", "g2v", "g2s", "g2c",
               "vm", "parr", "parb"]
              + ["tl%d" % i for i in range(8)] + ["pe%d" % i for i in range(9)] + ["ev%d" % i for i in range(9)])


def rank_program(g, core, T, topo):
    rank = T.rank_of(core)
    if rank is None:
        return
    cores = list(T.cores)
    n = len(cores)
    chips = []
    for c in cores:
        if topo.chip(c) not in chips:
            chips.append(topo.chip(c))
    nch = len(chips)
    chi = [chips.index(topo.chip(c)) for c in cores]
    dlt = [topo.die(c) for c in cores]
    assert nch == 8 and n == 16
    at = {}
    for r in range(n):
        at[(chi[r], dlt[r])] = r
    assert len(at) == n
    x, d = chi[rank], dlt[rank]
    for r in range(n):
        assert chi[r] == r % nch
        assert (dlt[r] == d) == (r // nch == rank // nch)
    partner = at[(x, 1 - d)]
    my = d * 64
    ot = (1 - d) * 64

    def slot_at(dst, src):
        return dlt[src] * 8 + ((chi[src] - chi[dst] - 1) % nch)

    def dst_id(r):
        rid, pid, _ = topo.addr(cores[r])
        return DstId(rid=rid, pnc=pid)

    def bits(m):
        return [1 << i for i in range(m.bit_length()) if (m >> i) & 1]

    far = [r for r in range(n) if chi[r] != x]
    far_mask = topo.mask(core, cores[partner])
    for r in far:
        assert topo.may_write(core, cores[r])
        far_mask &= topo.mask(core, cores[r])
    near_mask = topo.mask(core, cores[partner]) & ~far_mask
    nfar, nnear = len(bits(far_mask)), len(bits(near_mask))

    S = T.sem
    tot = {}

    def add(name, k):
        tot[name] = tot.get(name, 0) + k

    last = {}

    def op(q, key, make, name, free=False):
        if key in last and not free:
            q.wait_ge(S[last[key]], tot[last[key]])
        make().then_inc(S[name], 1)
        add(name, 1)
        last[key] = name

    V, A, P, Y = g.vector, g.scalar, g.tensor, g.sync
    Copy = ActivationFunctionType.Copy

    def vop(make, name, free=False):
        op(V, "v", make, name, free)

    def aop(make, name, free=False):
        op(A, "a", make, name, free)

    def vpick(out, win_end, off, name, free=False):
        vop(lambda: V.tensor_copy(out=out, in_=T.win[:, 0:win_end].indirect(off)), name, free)

    def apick(out, win_end, off, name, free=False):
        aop(lambda: A.activation(out=out, in_=T.win[:, 0:win_end].indirect(off), func=Copy), name, free)

    own = slot_at(rank, rank)
    Y.dma_start(T.lists[own * 128:(own + 1) * 128, :], T.idx[:]).then_inc(S.ownl, 16)
    add("ownl", 16)
    for k in range(8):
        q = Y if k % 2 == 0 else A
        q.dma_start(T.tabs[:, k * 256:(k + 1) * 256], T.tab[k * 512:(k + 1) * 512, :]).then_inc(S["tl%d" % k], 16)
        add("tl%d" % k, 16)

    vop(lambda: V.memset(T.ident[:], 1.0), "ones")
    g.iota(T.cst[:], [[16, 64]], ZC - ND * 128, 0).then_inc(S.gi, 1)
    g.iota(T.pj[:], [[128, 64]], 0, 1).then_inc(S.gi, 1)
    add("gi", 2)
    g.wait_ge(S.ones, 1)
    g.affine_select(T.ident[:], T.ident[:], [[-1, 128]], AluOpType.is_equal, 0.0, 0, 1).then_inc(S.gid, 1)
    add("gid", 1)
    V.wait_ge(S.gi, 2)
    vop(lambda: V.tensor_scalar(out=T.pj[:], in0=T.pj[:], scalar1=15, scalar2=None, op0=AluOpType.bitwise_and), "cs")
    vop(lambda: V.tensor_tensor(out=T.cst[:], in0=T.cst[:], in1=T.pj[:], op=AluOpType.add), "cs")

    g.wait_ge(S.ownl, 16)
    src = T.lists[own * 128:(own + 1) * 128, :]

    def lslot(r):
        k = slot_at(r, rank)
        return T.lists[k * 128:(k + 1) * 128, :]

    g.remote_dma_fused([
        RemoteDMATransfer(dst_ids=[dst_id(r) for r in far], dma_engine_mask=far_mask, remote_sem=S.larr,
                          srcs=[src], dsts=[lslot(r) for r in far]),
        RemoteDMATransfer(dst_ids=[dst_id(partner)], dma_engine_mask=near_mask, remote_sem=S.larr,
                          srcs=[src], dsts=[lslot(partner)]),
    ], local_sem=S.lsem)
    add("lsem", nfar + nnear)
    add("larr", nfar * len(far) + nnear)
    Y.wait_ge(S.ownl, 16)
    Y.wait_ge(S.larr, tot["larr"])
    Y.dma_start(T.xi[:], T.lists[:]).then_inc(S.xl, 16)
    add("xl", 16)

    bank = [0, 1, 2, 3, 4, 5, 0, 1, 2]
    P.wait_ge(S.gid, 1)

    def turn_unit(i):
        k = min(i, 7)
        if i < 8:
            P.wait_ge(S["tl%d" % k], 16)
        if i >= 6:
            P.wait_ge(S["ev%d" % (i - 6)], 4)
        ps = T["ps%d" % bank[i]]
        for m2 in ((0, 1) if i < 7 else (i - 7,)):
            o = ps[:, m2:256:2] if i < 7 else ps[:, 0:128]
            P.transpose(out=o, in_=T.tabs[:, k * 256 + m2 * 128:k * 256 + (m2 + 1) * 128],
                        identity=T.ident[:]).then_inc(S["pe%d" % i], 1)
            add("pe%d" % i, 1)

    def evac_unit(i, vector):
        k = min(i, 7)
        ps = T["ps%d" % bank[i]]
        (V if vector else A).wait_ge(S["pe%d" % i], tot["pe%d" % i])
        for h in range(2):
            for s in (h, 1 - h):
                fr = (h, s) != (0, 0)
                if i < 7:
                    o = T.win[s * 64:(s + 1) * 64, k * 512 + h:(k + 1) * 512:2]
                    a = ps[h * 64:(h + 1) * 64, 0:256]
                else:
                    o = T.win[s * 64:(s + 1) * 64, k * 512 + 2 * (i - 7) + h:(k + 1) * 512:4]
                    a = ps[h * 64:(h + 1) * 64, 0:128]
                if vector:
                    vop(lambda o=o, a=a: V.tensor_copy(out=o, in_=a), "ev%d" % i, fr)
                else:
                    aop(lambda o=o, a=a: A.activation(out=o, in_=a, func=Copy), "ev%d" % i, fr)

    for i in range(8):
        turn_unit(i)
    P.wait_ge(S.xrs, 8)
    P.transpose(out=T.ps6[:, 0:128], in_=T.xr[:], identity=T.ident[:]).then_inc(S.pidx, 1)
    add("pidx", 1)
    turn_unit(8)

    by_vector = (0, 2, 4, 8)
    for i in (0, 2, 4):
        evac_unit(i, True)
    for i in range(9):
        if i not in by_vector:
            evac_unit(i, False)

    V.wait_ge(S.xl, 16)
    for gr in range(8):
        vop(lambda gr=gr: V.tensor_copy(out=T.xr[:, gr * 16:(gr + 1) * 16], in_=T.xi[:, (gr // 4)::2]), "xrs",
            gr > 0)
    V.wait_ge(S.pidx, 1)
    vop(lambda: V.tensor_copy(out=T.vi[:], in_=T.ps6[:, 0:128]), "va")
    vop(lambda: V.tensor_scalar(out=T.pos[:], in0=T.vi[:], scalar1=4095, scalar2=None,
                                op0=AluOpType.bitwise_and), "va")
    vop(lambda: V.tensor_copy(out=T.offp[:], in_=T.pos[:]), "offps")
    evac_unit(8, True)
    for i in range(9):
        (A if i in by_vector else V).wait_ge(S["ev%d" % i], 4)
    A.wait_ge(S.offps, 1)

    c1 = ot + ND * 8
    ha = NA * 4
    cb = c1 + NA * 8
    vpick(T.g1[:, 0:ha * 16], ZC, T.offp[:, c1:c1 + ha], "g1v")
    apick(T.g1[:, ha * 16:NA * 128], ZC, T.offp[:, c1 + ha:cb], "g1s")
    vpick(T.gd[:, 0:ND * 128], ZC, T.offp[:, my:my + ND * 8], "gdv", True)
    apick(T.gd[:, ND * 128:2 * ND * 128], ZC, T.offp[:, ot:ot + ND * 8], "gds", True)
    apick(T.g1[:, NA * 128:NP * 128], ZC, T.offp[:, cb:ot + 64], "g1bs", True)

    rid, pid, _ = topo.addr(cores[partner])
    g.wait_ge(S.g1v, 1)
    g.wait_ge(S.g1s, 1)
    g.remote_dma(T.win[:, ZC:AC], T.g1[:, 0:NA * 128], S.parr, S.lsem, pid, rid, near_mask)
    add("lsem", nnear)
    add("parr", nnear)

    g.wait_ge(S.gdv, 1)
    g.wait_ge(S.gds, 1)
    eng = bits(far_mask)
    pair = [eng[2 * j] | eng[2 * j + 1] for j in range(len(eng) // 2)]

    def answer(r, first_slot, src_ap, mask):
        lm = (x - chi[r]) % nch
        c0 = ZC + (first_slot + lm) * 128
        k = len(bits(mask))
        add("lsem", k)
        add("aarr", k)
        return RemoteDMATransfer(dst_ids=[dst_id(r)], dma_engine_mask=mask, remote_sem=S.aarr, src=src_ap,
                                 dst=T.win[:, c0:c0 + 128])

    trs = []
    for q in range(ND):
        ch = (x + 1 + q) % nch
        trs.append(answer(at[(ch, d)], NP - 1, T.gd[:, q * 128:(q + 1) * 128], pair[2 * q]))
        trs.append(answer(at[(ch, 1 - d)], NP - 1 + ND, T.gd[:, (ND + q) * 128:(ND + q + 1) * 128], pair[2 * q + 1]))
    g.remote_dma_fused(trs, local_sem=S.lsem)

    g.wait_ge(S.g1bs, 1)
    g.remote_dma(T.win[:, AC:PC], T.g1[:, NA * 128:NP * 128], S.parb, S.lsem, pid, rid, near_mask)
    add("lsem", nnear)
    add("parb", nnear)

    m6 = 56
    vop(lambda: V.tensor_scalar(out=T.ow[:], in0=T.vi[:, my:my + 64], scalar1=12, scalar2=None,
                                op0=AluOpType.logical_shift_right), "vb", True)
    vop(lambda: V.tensor_scalar(out=T.notme[:], in0=T.ow[:], scalar1=rank, scalar2=BIG,
                                op0=AluOpType.not_equal, op1=AluOpType.mult), "vb")
    vop(lambda: V.tensor_tensor(out=T.dd[:], in0=T.notme[:], in1=T.pos[:, my:my + 64], op=AluOpType.add), "vb")
    vop(lambda: V.tensor_tensor(out=T.mn[:, 0:m6], in0=T.dd[:, 0:m6], in1=T.cst[:, 0:m6], op=AluOpType.min), "vb")
    vop(lambda: V.tensor_copy(out=T.offb[:], in_=T.mn[:, 0:m6]), "offbs")

    o0 = ND * 8
    V.wait_ge(S.parr, tot["parr"])
    vpick(T.g2[:, 0:256], AC, T.offb[:, o0:o0 + 16], "g2v")
    A.wait_ge(S.offbs, 1)
    A.wait_ge(S.parr, tot["parr"])
    apick(T.g2[:, 256:512], AC, T.offb[:, o0 + 16:o0 + 32], "g2s", True)
    A.wait_ge(S.parb, tot["parb"])
    apick(T.g2[:, 512:640], PC, T.offb[:, o0 + 32:o0 + 40], "g2c", True)
    g.wait_ge(S.g2v, 1)
    g.wait_ge(S.g2s, 1)
    g.remote_dma_fused([answer(at[((x + 1 + ND + j) % nch, d)], NP - 1, T.g2[:, j * 128:(j + 1) * 128], pair[j])
                        for j in range(4)], local_sem=S.lsem)
    g.wait_ge(S.g2c, 1)
    g.remote_dma_fused([answer(at[((x + 1 + ND + 4) % nch, d)], NP - 1, T.g2[:, 512:640], far_mask)], local_sem=S.lsem)

    me8 = slice(my + 56, my + 64)
    vop(lambda: V.tensor_scalar(out=T.lam[:], in0=T.vi[:, me8], scalar1=(nch - x) * 4096, scalar2=None,
                                op0=AluOpType.add), "vm")
    vop(lambda: V.tensor_scalar(out=T.lam[:], in0=T.lam[:], scalar1=12, scalar2=nch - 1,
                                op0=AluOpType.logical_shift_right, op1=AluOpType.bitwise_and), "vm")
    vop(lambda: V.tensor_scalar(out=T.hi[:], in0=T.vi[:, me8], scalar1=15, scalar2=None,
                                op0=AluOpType.logical_shift_right), "vm")
    vop(lambda: V.tensor_scalar(out=T.hi[:], in0=T.hi[:], scalar1=rank // nch, scalar2=ND,
                                op0=AluOpType.not_equal, op1=AluOpType.mult), "vm")
    vop(lambda: V.tensor_scalar(out=T.ge[:], in0=T.lam[:], scalar1=nch - ND, scalar2=None,
                                op0=AluOpType.is_ge), "vm")
    vop(lambda: V.tensor_tensor(out=T.ge[:], in0=T.ge[:], in1=T.hi[:], op=AluOpType.mult), "vm")
    vop(lambda: V.tensor_tensor(out=T.lam[:], in0=T.lam[:], in1=T.ge[:], op=AluOpType.add), "vm")
    vop(lambda: V.tensor_scalar(out=T.lam[:], in0=T.lam[:], scalar1=128, scalar2=None, op0=AluOpType.mult), "vm")
    vop(lambda: V.tensor_tensor(out=T.lam[:], in0=T.lam[:], in1=T.cst[:, 56:64], op=AluOpType.add), "vm")
    vop(lambda: V.tensor_tensor(out=T.hi[:], in0=T.dd[:, 56:64], in1=T.lam[:], op=AluOpType.min), "vm")
    vop(lambda: V.tensor_copy(out=T.offm[:], in_=T.hi[:]), "vm")

    V.wait_ge(S.parb, tot["parb"])
    V.wait_ge(S.aarr, tot["aarr"])
    vpick(T.rr[:], LC, T.offm[:], "rrs")
    P.wait_ge(S.rrs, 1)
    P.transpose(out=T.ps7[:, 0:128], in_=T.rr[:], identity=T.ident[:]).then_inc(S.pfin, 1)
    add("pfin", 1)
    V.wait_ge(S.pfin, 1)
    vop(lambda: V.tensor_copy(out=T.yy[:], in_=T.ps7[:, 0:128]), "yys")
    Y.wait_ge(S.yys, 1)
    Y.dma_start(T.y[0:128, :], T.yy[:, 0:64]).then_inc(S.st0, 16)
    add("st0", 16)
    A.wait_ge(S.yys, 1)
    A.dma_start(T.y[128:256, :], T.yy[:, 64:128]).then_inc(S.st1, 16)
    add("st1", 16)

    for name in SEMAPHORES:
        g.wait_ge(S[name], tot[name])
